import numpy as np
import ml_dtypes


def mxq(x, axis, fmt="e4m3"):
    dtype, down = {"e4m3": (ml_dtypes.float8_e4m3fn, 7), "e5m2": (ml_dtypes.float8_e5m2, 14)}[fmt]
    v = np.moveaxis(np.asarray(x, np.float32).astype(ml_dtypes.bfloat16).astype(np.float64), axis, -1)
    blocks = v.reshape(v.shape[:-1] + (-1, 32))
    amax = np.abs(blocks).max(-1, keepdims=True)
    byte = np.maximum(np.where(amax > 0, np.frexp(amax)[1] - 1 + 127, 0) - down, 1)
    scale = np.exp2(byte - 127.0)
    codes = (blocks / scale).astype(np.float32).astype(dtype).astype(np.float64)
    return np.moveaxis((codes * scale).reshape(v.shape), -1, axis)


WIDE = False


def mx_kscale(k):
    if not WIDE:
        return np.ones(k)
    levels = np.array([10, -10, 5, -5, 0])
    if k % 512:
        return np.exp2(np.random.permutation(np.resize(levels, k // 32))).repeat(32)
    a = np.empty((k // 512, 16))
    for p in range(k // 512):
        a[p, :8] = np.random.permutation(np.resize(levels, 8))
        for g in range(8):
            far = levels[np.abs(levels - a[p, g]) >= 10]
            a[p, g + 8] = far[np.random.randint(len(far))]
    return np.exp2(a.ravel()).repeat(32)


def f64(x):
    return np.asarray(x).astype(np.float64)


E2M1 = np.array([0.0, 0.5, 1.0, 1.5, 2.0, 3.0, 4.0, 6.0, -0.0, -0.5, -1.0, -1.5, -2.0, -3.0, -4.0, -6.0])


def pack_weight(w, fmt):
    k, n = w.shape
    w = f64(np.asarray(w, np.float32).astype(ml_dtypes.bfloat16)).reshape(k // 32, 32, n)
    amax = np.abs(w).max(1)
    if fmt == "e4m3":
        byte = np.frexp(amax)[1] - 1 + 127 - 7
    else:
        mant, ex = np.frexp(amax / 6.0)
        byte = np.where(mant > 0.5, ex, ex - 1) + 127
    byte = np.clip(np.where(amax > 0, byte, 1), 1, 254)
    scaled = (w * np.exp2(127.0 - byte)[:, None, :]).reshape(k, n).astype(np.float32)
    by_word = np.ascontiguousarray(scaled.reshape(k // 512, 128, 4, n).transpose(0, 1, 3, 2))
    if fmt == "e4m3":
        words = by_word.astype(ml_dtypes.float8_e4m3fn).view(np.uint8)
    else:
        c = by_word.astype(ml_dtypes.float4_e2m1fn).view(np.uint8) & 0xF
        words = (c[..., 0::2] | (c[..., 1::2] << 4)).reshape(k // 512, 128, 2 * n)
    return np.ascontiguousarray(words), np.ascontiguousarray(byte.astype(np.uint8).reshape(k // 512, 16, n))


def unpack_weight(words, scales, fmt):
    g, _, n = scales.shape
    words = np.ascontiguousarray(words).reshape(g, 128, n, -1)
    if fmt == "e4m3":
        vals = words.view(ml_dtypes.float8_e4m3fn).astype(np.float64)
    else:
        nib = np.empty((g, 128, n, 4), np.uint8)
        nib[..., 0::2] = words & 0xF
        nib[..., 1::2] = words >> 4
        vals = E2M1[nib]
    vals = vals * np.repeat(np.exp2(scales.astype(np.float64) - 127.0), 8, axis=1)[..., None]
    return vals.transpose(0, 1, 3, 2).reshape(g * 512, n)


def sigmoid(v):
    return 1.0 / (1.0 + np.exp(-v))


K, L, T, N = 1024, 1024, 512, 512


def setup_inputs():
    n = np.random.standard_normal
    fk = mx_kscale(K)
    fl = mx_kscale(L)
    xtp = pack_weight(n((K, T)) / fk[:, None], "e4m3")
    xqp = pack_weight(n((L, T)) / fl[:, None], "e2m1")
    wqp = pack_weight(n((L, N)) * 1 / np.sqrt(L) * fl[:, None], "e4m3")
    wcp = pack_weight(n((L, N)) * 1 / np.sqrt(L) * fl[:, None], "e2m1")
    return {
        "xt_words": xtp[0],
        "xt_scales": xtp[1],
        "wa": (n((K, N)) * 1 / np.sqrt(K) * fk[:, None]).astype(np.float32),
        "xq_words": xqp[0],
        "xq_scales": xqp[1],
        "wq_words": wqp[0],
        "wq_scales": wqp[1],
        "wc_words": wcp[0],
        "wc_scales": wcp[1],
    }


def reference(xt_words, xt_scales, wa, xq_words, xq_scales, wq_words, wq_scales, wc_words, wc_scales):
    xtu = unpack_weight(xt_words, xt_scales, "e4m3")
    xqu = unpack_weight(xq_words, xq_scales, "e2m1")
    wqu = unpack_weight(wq_words, wq_scales, "e4m3")
    wcu = unpack_weight(wc_words, wc_scales, "e2m1")
    waq = mxq(f64(wa), 0, "e4m3")
    z = waq.T @ xtu + wqu.T @ xqu
    zp = np.pad(z, ((0, 0), (1, 0)))[:, :T]
    s = wcu.T @ xqu
    y = z * sigmoid(zp) + 0.5 * s
    return y

@@ -1,0 +1,212 @@
+from contextlib import ExitStack
+
+import concourse.mybir as mybir
+
+K, L, T, N = 1024, 1024, 512, 512
+FLOPS = 2 * N * T * (K + 2 * L)
+
+F32 = mybir.dt.float32
+BF16 = mybir.dt.bfloat16
+I32 = mybir.dt.int32
+U32 = mybir.dt.uint32
+U8 = mybir.dt.uint8
+FP8X4 = mybir.dt.float8_e4m3fn_x4
+FP4X4 = mybir.dt.float4_e2m1fn_x4
+ACT = mybir.ActivationFunctionType
+ALU = mybir.AluOpType
+
+P = 128
+PACK = 4
+K_PASS = P * PACK
+PASSES = K // K_PASS
+TILES = N // P
+GATE_PAD = 4
+
+
+def tile_mix_sum_and_its_own_gate_kernel(
+    tc, xt_words, xt_scales, wa, xq_words, xq_scales, wq_words, wq_scales, wc_words, wc_scales, out
+):
+    nc = tc.nc
+    with ExitStack() as ctx:
+        sb = ctx.enter_context(tc.tile_pool(name="sb", bufs=1))
+        ps = ctx.enter_context(tc.psum_pool(name="ps", bufs=1))
+        ctx.enter_context(tc.manual_schedule())
+
+        def plane(name, engine):
+            t = sb.tile([P, PASSES * 512], U8, name=name, align_bytes=64)
+            engine.memset(t[:].bitcast(U32), 0)
+            return t
+
+        def load_scale(queue, t, scales, r):
+            queue.dma_start(
+                out=t[r:P:32, :].bitcast(I32).rearrange("q (z c) -> q z c", z=PASSES),
+                in_=scales.bitcast(I32).rearrange("z (q r) c -> r q z c", r=4)[r],
+            )
+
+        def load_fp8(queue, name, words, c0, c1):
+            t = sb.tile([P, PASSES, c1 - c0], U32, name=name, align_bytes=64)
+            src = words.rearrange("z p c r -> p z (c r)")[:, :, 4 * c0 : 4 * c1].bitcast(I32)
+            queue.dma_start(out=t[:].bitcast(I32), in_=src)
+            return t
+
+        def load_fp4(queue, name, words, c0, c1):
+            t = sb.tile([P, PASSES, 2 * (c1 - c0)], U8, name=name, align_bytes=64)
+            src = words.rearrange("z p b -> p z b")[:, :, 2 * c0 : 2 * c1].bitcast(I32)
+            queue.dma_start(out=t[:].bitcast(I32), in_=src)
+            return t
+
+        raw, grouped, codes, cscales = {}, {}, {}, {}
+
+        def load_wa(queue, c0, c1, g):
+            t = sb.tile([P, PACK, c1 - c0], F32, name="raw%d_%d" % (c0, g))
+            rows = wa[g * K_PASS : (g + 1) * K_PASS, c0:c1]
+            queue.dma_start(out=t[:], in_=rows.rearrange("(p j) c -> p j c", j=PACK))
+            raw[c0, g] = t
+
+        def cast(engine, c0, g):
+            src = raw[c0, g]
+            w = src.shape[2]
+            t = sb.tile([P, w * PACK], BF16, name="grp%d_%d" % (c0, g), align_bytes=64)
+            dst_v = t[:].rearrange("p (c i j) -> p c j i", i=2, j=PACK)
+            src_v = src[:].rearrange("p j (c i) -> p c j i", i=2)
+            if engine == "v":
+                nc.vector.tensor_copy(out=dst_v, in_=src_v)
+            else:
+                nc.scalar.copy(out=dst_v, in_=src_v)
+            grouped[c0, g] = t
+
+        def quant(c0, g):
+            src = grouped[c0, g]
+            w = src.shape[1] // PACK
+            cw = sb.tile([P, w], U32, name="cod%d_%d" % (c0, g), align_bytes=64)
+            cs = sb.tile([P, w], U8, name="csc%d_%d" % (c0, g), align_bytes=64)
+            nc.vector.quantize_mx(out=cw[:].bitcast(FP8X4), scales=cs[:], in_=src[:])
+            for i in range(c0 // P, (c0 + w) // P):
+                o = i * P - c0
+                codes[i, g] = cw[:, o : o + P]
+                cscales[i, g] = cs[:, o : o + P]
+
+        z, s, gate, prod, wqt, wct = {}, {}, {}, {}, {}, {}
+        for i in range(TILES):
+            z[i] = ps.tile([P, T], F32, name="z%d" % i)
+            s[i] = ps.tile([P, T], F32, name="s%d" % i)
+            gate[i] = sb.tile([P, GATE_PAD + T], F32, name="gate%d" % i)
+            prod[i] = sb.tile([P, T], F32, name="prod%d" % i)
+
+        def mm_q(i, g):
+            t, o = wqt[i]
+            nc.tensor.matmul_mx(
+                out=z[i][:],
+                lhsT=t[:, g, o : o + P].bitcast(FP8X4),
+                lhsT_scale=wq_s[:, g * N + i * P : g * N + (i + 1) * P],
+                rhs=xq[:, g, :].bitcast(FP4X4),
+                rhs_scale=xq_s[:, g * T : (g + 1) * T],
+                start=(g == 0),
+                stop=False,
+            )
+
+        def mm_a(i, g):
+            nc.tensor.matmul_mx(
+                out=z[i][:],
+                lhsT=codes[i, g].bitcast(FP8X4),
+                lhsT_scale=cscales[i, g],
+                rhs=xt[:, g, :].bitcast(FP8X4),
+                rhs_scale=xt_s[:, g * T : (g + 1) * T],
+                start=False,
+                stop=(g == PASSES - 1),
+            )
+
+        def mm_s(i, g):
+            t, o = wct[i]
+            nc.tensor.matmul_mx(
+                out=s[i][:],
+                lhsT=t[:, g, 2 * o : 2 * (o + P)].bitcast(FP4X4),
+                lhsT_scale=wc_s[:, g * N + i * P : g * N + (i + 1) * P],
+                rhs=xq[:, g, :].bitcast(FP4X4),
+                rhs_scale=xq_s[:, g * T : (g + 1) * T],
+                start=(g == 0),
+                stop=(g == PASSES - 1),
+            )
+
+        def sig(i):
+            nc.scalar.activation(out=gate[i][:, GATE_PAD:], in_=z[i][:], func=ACT.Sigmoid)
+
+        def mul(i):
+            nc.vector.tensor_tensor(
+                out=prod[i][:], in0=z[i][:], in1=gate[i][:, GATE_PAD - 1 : GATE_PAD - 1 + T], op=ALU.mult
+            )
+
+        def add(i, t0=0, t1=T, queue=nc.sync):
+            y = sb.tile([P, t1 - t0], F32, name="y%d_%d" % (i, t0))
+            nc.vector.scalar_tensor_tensor(
+                out=y[:], in0=s[i][:, t0:t1], scalar=0.5, in1=prod[i][:, t0:t1], op0=ALU.mult, op1=ALU.add
+            )
+            queue.dma_start(out=out[i * P : (i + 1) * P, t0:t1], in_=y[:])
+
+        def both(f, i):
+            for g in range(PASSES):
+                f(i, g)
+
+        xq_s = plane("xq_s", nc.vector)
+        wq_s = plane("wq_s", nc.vector)
+        wc_s = plane("wc_s", nc.vector)
+        xt_s = plane("xt_s", nc.vector)
+        zero = sb.tile([P, 1], F32, name="zero")
+        nc.vector.memset(zero[:], 0.0)
+        for i in range(TILES):
+            nc.scalar.activation(out=gate[i][:, GATE_PAD - 1 : GATE_PAD], in_=zero[:], func=ACT.Sigmoid)
+        for r in range(4):
+            load_scale(nc.scalar, xt_s, xt_scales, r)
+
+        load_wa(nc.sync, 0, 256, 0)
+        xq = load_fp4(nc.sync, "xq", xq_words, 0, T)
+        for r in range(4):
+            load_scale(nc.sync, xq_s, xq_scales, r)
+        wq = load_fp8(nc.sync, "wq", wq_words, 0, N)
+        for r in range(4):
+            load_scale(nc.sync, wq_s, wq_scales, r)
+        load_wa(nc.sync, 0, 256, 1)
+        xt = load_fp8(nc.sync, "xt", xt_words, 0, T)
+        wc = load_fp4(nc.sync, "wc", wc_words, 0, N)
+        for r in range(4):
+            load_scale(nc.sync, wc_s, wc_scales, r)
+        for c0 in (256, 384):
+            for g in range(PASSES):
+                load_wa(nc.sync, c0, c0 + P, g)
+        for i in range(TILES):
+            wqt[i] = (wq, i * P)
+            wct[i] = (wc, i * P)
+
+        for g in range(PASSES):
+            cast("v", 0, g)
+            quant(0, g)
+        for i in range(TILES):
+            both(mm_q, i)
+        both(mm_a, 0)
+        sig(0)
+        both(mm_a, 1)
+        both(mm_s, 0)
+        both(mm_s, 1)
+        both(mm_s, 2)
+        mul(0)
+        cast("s", 256, 0)
+        sig(1)
+        cast("v", 256, 1)
+        add(0)
+        quant(256, 0)
+        quant(256, 1)
+        both(mm_a, 2)
+        both(mm_s, 3)
+        cast("s", 384, 0)
+        sig(2)
+        mul(1)
+        cast("v", 384, 1)
+        add(1)
+        quant(384, 0)
+        quant(384, 1)
+        both(mm_a, 3)
+        sig(3)
+        mul(2)
+        mul(3)
+        add(2)
+        add(3)

@@ -20,6 +20,9 @@ PACK = 4
 K_PASS = P * PACK
 PASSES = K // K_PASS
 TILES = N // P
+PAIR = 2
+QUADRANT = 32
+SCALE_ROWS = 4
 GATE_PAD = 4
 
 
@@ -32,181 +35,145 @@ def tile_mix_sum_and_its_own_gate_kernel(
         ps = ctx.enter_context(tc.psum_pool(name="ps", bufs=1))
         ctx.enter_context(tc.manual_schedule())
 
-        def plane(name, engine):
-            t = sb.tile([P, PASSES * 512], U8, name=name, align_bytes=64)
-            engine.memset(t[:].bitcast(U32), 0)
-            return t
+        def new_plane(name, engine):
+            plane = sb.tile([P, PASSES * T], U8, name=name, align_bytes=64)
+            engine.memset(plane[:].bitcast(U32), 0)
+            return plane
 
-        def load_scale(queue, t, scales, r):
-            queue.dma_start(
-                out=t[r:P:32, :].bitcast(I32).rearrange("q (z c) -> q z c", z=PASSES),
-                in_=scales.bitcast(I32).rearrange("z (q r) c -> r q z c", r=4)[r],
-            )
+        def load_scales(queue, plane, scales):
+            rows = scales.bitcast(I32).rearrange("g (q r) c -> r q g c", r=SCALE_ROWS)
+            for r in range(SCALE_ROWS):
+                dst = plane[r:P:QUADRANT, :].bitcast(I32).rearrange("q (g c) -> q g c", g=PASSES)
+                queue.dma_start(out=dst, in_=rows[r])
 
-        def load_fp8(queue, name, words, c0, c1):
-            t = sb.tile([P, PASSES, c1 - c0], U32, name=name, align_bytes=64)
-            src = words.rearrange("z p c r -> p z (c r)")[:, :, 4 * c0 : 4 * c1].bitcast(I32)
-            queue.dma_start(out=t[:].bitcast(I32), in_=src)
-            return t
+        def load_bytes(name, src):
+            words = sb.tile(list(src.shape), U8, name=name, align_bytes=64)
+            nc.sync.dma_start(out=words[:].bitcast(I32), in_=src.bitcast(I32))
+            return words
 
-        def load_fp4(queue, name, words, c0, c1):
-            t = sb.tile([P, PASSES, 2 * (c1 - c0)], U8, name=name, align_bytes=64)
-            src = words.rearrange("z p b -> p z b")[:, :, 2 * c0 : 2 * c1].bitcast(I32)
-            queue.dma_start(out=t[:].bitcast(I32), in_=src)
-            return t
+        def load_wa(g):
+            rows = sb.tile([P, PACK, N], F32, name="wa_rows%d" % g)
+            src = wa[g * K_PASS : (g + 1) * K_PASS, :].rearrange("(p j) n -> p j n", j=PACK)
+            nc.sync.dma_start(out=rows[:], in_=src)
+            return rows
 
-        raw, grouped, codes, cscales = {}, {}, {}, {}
+        z = [ps.tile([P, T], F32, name="z%d" % i) for i in range(TILES)]
+        s = [ps.tile([P, T], F32, name="s%d" % i) for i in range(TILES)]
+        gate = [sb.tile([P, GATE_PAD + T], F32, name="gate%d" % i) for i in range(TILES)]
+        gated = [sb.tile([P, T], F32, name="gated%d" % i) for i in range(TILES)]
 
-        def load_wa(queue, c0, c1, g):
-            t = sb.tile([P, PACK, c1 - c0], F32, name="raw%d_%d" % (c0, g))
-            rows = wa[g * K_PASS : (g + 1) * K_PASS, c0:c1]
-            queue.dma_start(out=t[:], in_=rows.rearrange("(p j) c -> p j c", j=PACK))
-            raw[c0, g] = t
+        wq_plane = new_plane("wq_plane", nc.gpsimd)
+        wc_plane = new_plane("wc_plane", nc.gpsimd)
+        xq_plane = new_plane("xq_plane", nc.vector)
+        xt_plane = new_plane("xt_plane", nc.vector)
+        load_scales(nc.gpsimd, wq_plane, wq_scales)
+        load_scales(nc.gpsimd, wc_plane, wc_scales)
 
-        def cast(engine, c0, g):
-            src = raw[c0, g]
-            w = src.shape[2]
-            t = sb.tile([P, w * PACK], BF16, name="grp%d_%d" % (c0, g), align_bytes=64)
-            dst_v = t[:].rearrange("p (c i j) -> p c j i", i=2, j=PACK)
-            src_v = src[:].rearrange("p j (c i) -> p c j i", i=2)
-            if engine == "v":
-                nc.vector.tensor_copy(out=dst_v, in_=src_v)
-            else:
-                nc.scalar.copy(out=dst_v, in_=src_v)
-            grouped[c0, g] = t
-
-        def quant(c0, g):
-            src = grouped[c0, g]
-            w = src.shape[1] // PACK
-            cw = sb.tile([P, w], U32, name="cod%d_%d" % (c0, g), align_bytes=64)
-            cs = sb.tile([P, w], U8, name="csc%d_%d" % (c0, g), align_bytes=64)
-            nc.vector.quantize_mx(out=cw[:].bitcast(FP8X4), scales=cs[:], in_=src[:])
-            for i in range(c0 // P, (c0 + w) // P):
-                o = i * P - c0
-                codes[i, g] = cw[:, o : o + P]
-                cscales[i, g] = cs[:, o : o + P]
-
-        z, s, gate, prod, wqt, wct = {}, {}, {}, {}, {}, {}
-        for i in range(TILES):
-            z[i] = ps.tile([P, T], F32, name="z%d" % i)
-            s[i] = ps.tile([P, T], F32, name="s%d" % i)
-            gate[i] = sb.tile([P, GATE_PAD + T], F32, name="gate%d" % i)
-            prod[i] = sb.tile([P, T], F32, name="prod%d" % i)
-
-        def mm_q(i, g):
-            t, o = wqt[i]
-            nc.tensor.matmul_mx(
-                out=z[i][:],
-                lhsT=t[:, g, o : o + P].bitcast(FP8X4),
-                lhsT_scale=wq_s[:, g * N + i * P : g * N + (i + 1) * P],
-                rhs=xq[:, g, :].bitcast(FP4X4),
-                rhs_scale=xq_s[:, g * T : (g + 1) * T],
-                start=(g == 0),
-                stop=False,
-            )
-
-        def mm_a(i, g):
-            nc.tensor.matmul_mx(
-                out=z[i][:],
-                lhsT=codes[i, g].bitcast(FP8X4),
-                lhsT_scale=cscales[i, g],
-                rhs=xt[:, g, :].bitcast(FP8X4),
-                rhs_scale=xt_s[:, g * T : (g + 1) * T],
-                start=False,
-                stop=(g == PASSES - 1),
-            )
-
-        def mm_s(i, g):
-            t, o = wct[i]
-            nc.tensor.matmul_mx(
-                out=s[i][:],
-                lhsT=t[:, g, 2 * o : 2 * (o + P)].bitcast(FP4X4),
-                lhsT_scale=wc_s[:, g * N + i * P : g * N + (i + 1) * P],
-                rhs=xq[:, g, :].bitcast(FP4X4),
-                rhs_scale=xq_s[:, g * T : (g + 1) * T],
-                start=(g == 0),
-                stop=(g == PASSES - 1),
-            )
-
-        def sig(i):
-            nc.scalar.activation(out=gate[i][:, GATE_PAD:], in_=z[i][:], func=ACT.Sigmoid)
-
-        def mul(i):
-            nc.vector.tensor_tensor(
-                out=prod[i][:], in0=z[i][:], in1=gate[i][:, GATE_PAD - 1 : GATE_PAD - 1 + T], op=ALU.mult
-            )
-
-        def add(i, t0=0, t1=T, queue=nc.sync):
-            y = sb.tile([P, t1 - t0], F32, name="y%d_%d" % (i, t0))
-            nc.vector.scalar_tensor_tensor(
-                out=y[:], in0=s[i][:, t0:t1], scalar=0.5, in1=prod[i][:, t0:t1], op0=ALU.mult, op1=ALU.add
-            )
-            queue.dma_start(out=out[i * P : (i + 1) * P, t0:t1], in_=y[:])
-
-        def both(f, i):
-            for g in range(PASSES):
-                f(i, g)
-
-        xq_s = plane("xq_s", nc.vector)
-        wq_s = plane("wq_s", nc.vector)
-        wc_s = plane("wc_s", nc.vector)
-        xt_s = plane("xt_s", nc.vector)
         zero = sb.tile([P, 1], F32, name="zero")
         nc.vector.memset(zero[:], 0.0)
         for i in range(TILES):
             nc.scalar.activation(out=gate[i][:, GATE_PAD - 1 : GATE_PAD], in_=zero[:], func=ACT.Sigmoid)
-        for r in range(4):
-            load_scale(nc.scalar, xt_s, xt_scales, r)
 
-        load_wa(nc.sync, 0, 256, 0)
-        xq = load_fp4(nc.sync, "xq", xq_words, 0, T)
-        for r in range(4):
-            load_scale(nc.sync, xq_s, xq_scales, r)
-        wq = load_fp8(nc.sync, "wq", wq_words, 0, N)
-        for r in range(4):
-            load_scale(nc.sync, wq_s, wq_scales, r)
-        load_wa(nc.sync, 0, 256, 1)
-        xt = load_fp8(nc.sync, "xt", xt_words, 0, T)
-        wc = load_fp4(nc.sync, "wc", wc_words, 0, N)
-        for r in range(4):
-            load_scale(nc.sync, wc_s, wc_scales, r)
-        for c0 in (256, 384):
+        wq = load_bytes("wq", wq_words.rearrange("g p n j -> p g (n j)"))
+        load_scales(nc.sync, xq_plane, xq_scales)
+        xq = load_bytes("xq", xq_words.rearrange("g p b -> p g b"))
+        wa_rows = [load_wa(g) for g in range(PASSES)]
+        load_scales(nc.sync, xt_plane, xt_scales)
+        xt = [load_bytes("xt%d" % g, xt_words[g].rearrange("p t j -> p (t j)")) for g in range(PASSES)]
+        wc = load_bytes("wc", wc_words.rearrange("g p b -> p g b"))
+
+        wa_codes, wa_planes = {}, {}
+
+        def quantise_wa(g, scalar_tiles):
+            grouped = [
+                sb.tile([P, PAIR * K_PASS], BF16, name="wa_grouped%d_%d" % (g, h), align_bytes=64)
+                for h in range(TILES // PAIR)
+            ]
+            for i in range(TILES):
+                h, u = divmod(i, PAIR)
+                dst = grouped[h][:, u * K_PASS : (u + 1) * K_PASS].rearrange("p (c e j) -> p c j e", e=2, j=PACK)
+                src = wa_rows[g][:, :, i * P : (i + 1) * P].rearrange("p j (c e) -> p c j e", e=2)
+                if i in scalar_tiles:
+                    nc.scalar.copy(out=dst, in_=src)
+                else:
+                    nc.vector.tensor_copy(out=dst, in_=src)
+            for h in range(TILES // PAIR):
+                codes = sb.tile([P, PAIR * P], U32, name="wa_codes%d_%d" % (g, h), align_bytes=64)
+                plane = sb.tile([P, PAIR * P], U8, name="wa_plane%d_%d" % (g, h), align_bytes=64)
+                nc.vector.quantize_mx(out=codes[:].bitcast(FP8X4), scales=plane[:], in_=grouped[h][:])
+                for u in range(PAIR):
+                    wa_codes[h * PAIR + u, g] = codes[:, u * P : (u + 1) * P]
+                    wa_planes[h * PAIR + u, g] = plane[:, u * P : (u + 1) * P]
+
+        def plane_cols(plane, g, first, width):
+            return plane[:, g * T + first : g * T + first + width]
+
+        def wq_xq(i):
             for g in range(PASSES):
-                load_wa(nc.sync, c0, c0 + P, g)
-        for i in range(TILES):
-            wqt[i] = (wq, i * P)
-            wct[i] = (wc, i * P)
+                nc.tensor.matmul_mx(
+                    out=z[i][:],
+                    lhsT=wq[:, g, 4 * i * P : 4 * (i + 1) * P].bitcast(FP8X4),
+                    lhsT_scale=plane_cols(wq_plane, g, i * P, P),
+                    rhs=xq[:, g, :].bitcast(FP4X4),
+                    rhs_scale=plane_cols(xq_plane, g, 0, T),
+                    start=(g == 0),
+                    stop=False,
+                )
 
-        for g in range(PASSES):
-            cast("v", 0, g)
-            quant(0, g)
+        def wa_xt(i, g):
+            nc.tensor.matmul_mx(
+                out=z[i][:],
+                lhsT=wa_codes[i, g].bitcast(FP8X4),
+                lhsT_scale=wa_planes[i, g],
+                rhs=xt[g][:].bitcast(FP8X4),
+                rhs_scale=plane_cols(xt_plane, g, 0, T),
+                start=False,
+                stop=(g == PASSES - 1),
+            )
+            if g == PASSES - 1:
+                nc.scalar.activation(out=gate[i][:, GATE_PAD:], in_=z[i][:], func=ACT.Sigmoid)
+
+        def wc_xq(i):
+            for g in range(PASSES):
+                nc.tensor.matmul_mx(
+                    out=s[i][:],
+                    lhsT=wc[:, g, 2 * i * P : 2 * (i + 1) * P].bitcast(FP4X4),
+                    lhsT_scale=plane_cols(wc_plane, g, i * P, P),
+                    rhs=xq[:, g, :].bitcast(FP4X4),
+                    rhs_scale=plane_cols(xq_plane, g, 0, T),
+                    start=(g == 0),
+                    stop=(g == PASSES - 1),
+                )
+
+        def apply_gate(i):
+            shifted = gate[i][:, GATE_PAD - 1 : GATE_PAD - 1 + T]
+            nc.vector.tensor_tensor(out=gated[i][:], in0=z[i][:], in1=shifted, op=ALU.mult)
+
+        def add_and_store(i, t0, t1):
+            y = sb.tile([P, t1 - t0], F32, name="y%d_%d" % (i, t0))
+            nc.vector.scalar_tensor_tensor(
+                out=y[:], in0=s[i][:, t0:t1], scalar=0.5, in1=gated[i][:, t0:t1], op0=ALU.mult, op1=ALU.add
+            )
+            nc.sync.dma_start(out=out[i * P : (i + 1) * P, t0:t1], in_=y[:])
+
+        quantise_wa(0, scalar_tiles=(3,))
+        quantise_wa(1, scalar_tiles=(1, 3))
+
         for i in range(TILES):
-            both(mm_q, i)
-        both(mm_a, 0)
-        sig(0)
-        both(mm_a, 1)
-        both(mm_s, 0)
-        both(mm_s, 1)
-        both(mm_s, 2)
-        mul(0)
-        cast("s", 256, 0)
-        sig(1)
-        cast("v", 256, 1)
-        add(0)
-        quant(256, 0)
-        quant(256, 1)
-        both(mm_a, 2)
-        both(mm_s, 3)
-        cast("s", 384, 0)
-        sig(2)
-        mul(1)
-        cast("v", 384, 1)
-        add(1)
-        quant(384, 0)
-        quant(384, 1)
-        both(mm_a, 3)
-        sig(3)
-        mul(2)
-        mul(3)
-        add(2)
-        add(3)
+            wq_xq(i)
+        for g in range(PASSES):
+            for i in range(PAIR):
+                wa_xt(i, g)
+        for i in range(PAIR, TILES):
+            for g in range(PASSES):
+                wa_xt(i, g)
+            wc_xq(i - PAIR)
+        for i in range(TILES - PAIR, TILES):
+            wc_xq(i)
+
+        apply_gate(0)
+        for i in range(1, TILES):
+            apply_gate(i)
+            add_and_store(i - 1, 0, T)
+        add_and_store(TILES - 1, 0, T // 2)
+        add_and_store(TILES - 1, T // 2, T)

@@ -40,11 +40,11 @@ def tile_mix_sum_and_its_own_gate_kernel(
             engine.memset(plane[:].bitcast(U32), 0)
             return plane
 
-        def load_scales(queue, plane, scales):
+        def load_scales(plane, scales):
             rows = scales.bitcast(I32).rearrange("g (q r) c -> r q g c", r=SCALE_ROWS)
             for r in range(SCALE_ROWS):
                 dst = plane[r:P:QUADRANT, :].bitcast(I32).rearrange("q (g c) -> q g c", g=PASSES)
-                queue.dma_start(out=dst, in_=rows[r])
+                nc.sync.dma_start(out=dst, in_=rows[r])
 
         def load_bytes(name, src):
             words = sb.tile(list(src.shape), U8, name=name, align_bytes=64)
@@ -62,29 +62,34 @@ def tile_mix_sum_and_its_own_gate_kernel(
         gate = [sb.tile([P, GATE_PAD + T], F32, name="gate%d" % i) for i in range(TILES)]
         gated = [sb.tile([P, T], F32, name="gated%d" % i) for i in range(TILES)]
 
+        xt_plane = new_plane("xt_plane", nc.vector)
+        xq_plane = new_plane("xq_plane", nc.vector)
         wq_plane = new_plane("wq_plane", nc.gpsimd)
         wc_plane = new_plane("wc_plane", nc.gpsimd)
-        xq_plane = new_plane("xq_plane", nc.vector)
-        xt_plane = new_plane("xt_plane", nc.vector)
-        load_scales(nc.gpsimd, wq_plane, wq_scales)
-        load_scales(nc.gpsimd, wc_plane, wc_scales)
 
         zero = sb.tile([P, 1], F32, name="zero")
         nc.vector.memset(zero[:], 0.0)
         for i in range(TILES):
             nc.scalar.activation(out=gate[i][:, GATE_PAD - 1 : GATE_PAD], in_=zero[:], func=ACT.Sigmoid)
 
-        wq = load_bytes("wq", wq_words.rearrange("g p n j -> p g (n j)"))
-        load_scales(nc.sync, xq_plane, xq_scales)
+        xt, wa_rows, wq = {}, {}, {}
+        xt[0] = load_bytes("xt0", xt_words[0].rearrange("p t j -> p (t j)"))
+        load_scales(xt_plane, xt_scales)
+        wa_rows[0] = load_wa(0)
+        load_scales(xq_plane, xq_scales)
+        wa_rows[1] = load_wa(1)
+        load_scales(wq_plane, wq_scales)
+        xt[1] = load_bytes("xt1", xt_words[1].rearrange("p t j -> p (t j)"))
         xq = load_bytes("xq", xq_words.rearrange("g p b -> p g b"))
-        wa_rows = [load_wa(g) for g in range(PASSES)]
-        load_scales(nc.sync, xt_plane, xt_scales)
-        xt = [load_bytes("xt%d" % g, xt_words[g].rearrange("p t j -> p (t j)")) for g in range(PASSES)]
+        for h in range(TILES // PAIR):
+            cols = wq_words[:, :, h * PAIR * P : (h + 1) * PAIR * P, :]
+            wq[h] = load_bytes("wq%d" % h, cols.rearrange("g p n j -> p g (n j)"))
+        load_scales(wc_plane, wc_scales)
         wc = load_bytes("wc", wc_words.rearrange("g p b -> p g b"))
 
         wa_codes, wa_planes = {}, {}
 
-        def quantise_wa(g, scalar_tiles):
+        def quantise_wa(g):
             grouped = [
                 sb.tile([P, PAIR * K_PASS], BF16, name="wa_grouped%d_%d" % (g, h), align_bytes=64)
                 for h in range(TILES // PAIR)
@@ -93,10 +98,10 @@ def tile_mix_sum_and_its_own_gate_kernel(
                 h, u = divmod(i, PAIR)
                 dst = grouped[h][:, u * K_PASS : (u + 1) * K_PASS].rearrange("p (c e j) -> p c j e", e=2, j=PACK)
                 src = wa_rows[g][:, :, i * P : (i + 1) * P].rearrange("p j (c e) -> p c j e", e=2)
-                if i in scalar_tiles:
-                    nc.scalar.copy(out=dst, in_=src)
-                else:
+                if u == 0:
                     nc.vector.tensor_copy(out=dst, in_=src)
+                else:
+                    nc.scalar.copy(out=dst, in_=src)
             for h in range(TILES // PAIR):
                 codes = sb.tile([P, PAIR * P], U32, name="wa_codes%d_%d" % (g, h), align_bytes=64)
                 plane = sb.tile([P, PAIR * P], U8, name="wa_plane%d_%d" % (g, h), align_bytes=64)
@@ -108,18 +113,6 @@ def tile_mix_sum_and_its_own_gate_kernel(
         def plane_cols(plane, g, first, width):
             return plane[:, g * T + first : g * T + first + width]
 
-        def wq_xq(i):
-            for g in range(PASSES):
-                nc.tensor.matmul_mx(
-                    out=z[i][:],
-                    lhsT=wq[:, g, 4 * i * P : 4 * (i + 1) * P].bitcast(FP8X4),
-                    lhsT_scale=plane_cols(wq_plane, g, i * P, P),
-                    rhs=xq[:, g, :].bitcast(FP4X4),
-                    rhs_scale=plane_cols(xq_plane, g, 0, T),
-                    start=(g == 0),
-                    stop=False,
-                )
-
         def wa_xt(i, g):
             nc.tensor.matmul_mx(
                 out=z[i][:],
@@ -127,11 +120,23 @@ def tile_mix_sum_and_its_own_gate_kernel(
                 lhsT_scale=wa_planes[i, g],
                 rhs=xt[g][:].bitcast(FP8X4),
                 rhs_scale=plane_cols(xt_plane, g, 0, T),
-                start=False,
-                stop=(g == PASSES - 1),
+                start=(g == 0),
+                stop=False,
             )
-            if g == PASSES - 1:
-                nc.scalar.activation(out=gate[i][:, GATE_PAD:], in_=z[i][:], func=ACT.Sigmoid)
+
+        def wq_xq(i):
+            h, u = divmod(i, PAIR)
+            for g in range(PASSES):
+                nc.tensor.matmul_mx(
+                    out=z[i][:],
+                    lhsT=wq[h][:, g, 4 * u * P : 4 * (u + 1) * P].bitcast(FP8X4),
+                    lhsT_scale=plane_cols(wq_plane, g, i * P, P),
+                    rhs=xq[:, g, :].bitcast(FP4X4),
+                    rhs_scale=plane_cols(xq_plane, g, 0, T),
+                    start=False,
+                    stop=(g == PASSES - 1),
+                )
+            nc.scalar.activation(out=gate[i][:, GATE_PAD:], in_=z[i][:], func=ACT.Sigmoid)
 
         def wc_xq(i):
             for g in range(PASSES):
@@ -145,9 +150,9 @@ def tile_mix_sum_and_its_own_gate_kernel(
                     stop=(g == PASSES - 1),
                 )
 
-        def apply_gate(i):
-            shifted = gate[i][:, GATE_PAD - 1 : GATE_PAD - 1 + T]
-            nc.vector.tensor_tensor(out=gated[i][:], in0=z[i][:], in1=shifted, op=ALU.mult)
+        def apply_gate(i, t0, t1):
+            shifted = gate[i][:, GATE_PAD - 1 + t0 : GATE_PAD - 1 + t1]
+            nc.vector.tensor_tensor(out=gated[i][:, t0:t1], in0=z[i][:, t0:t1], in1=shifted, op=ALU.mult)
 
         def add_and_store(i, t0, t1):
             y = sb.tile([P, t1 - t0], F32, name="y%d_%d" % (i, t0))
@@ -156,24 +161,26 @@ def tile_mix_sum_and_its_own_gate_kernel(
             )
             nc.sync.dma_start(out=out[i * P : (i + 1) * P, t0:t1], in_=y[:])
 
-        quantise_wa(0, scalar_tiles=(3,))
-        quantise_wa(1, scalar_tiles=(1, 3))
-
-        for i in range(TILES):
-            wq_xq(i)
         for g in range(PASSES):
-            for i in range(PAIR):
+            quantise_wa(g)
+            for i in range(TILES):
                 wa_xt(i, g)
-        for i in range(PAIR, TILES):
-            for g in range(PASSES):
-                wa_xt(i, g)
-            wc_xq(i - PAIR)
-        for i in range(TILES - PAIR, TILES):
+
+        last = TILES - 1
+        for i in range(last):
+            wq_xq(i)
+        wc_xq(0)
+        wq_xq(last)
+        for i in range(1, TILES):
             wc_xq(i)
 
-        apply_gate(0)
-        for i in range(1, TILES):
-            apply_gate(i)
+        apply_gate(0, 0, T)
+        for i in range(1, last):
+            apply_gate(i, 0, T)
             add_and_store(i - 1, 0, T)
-        add_and_store(TILES - 1, 0, T // 2)
-        add_and_store(TILES - 1, T // 2, T)
+        add_and_store(last - 1, 0, T)
+        halves = ((0, T // 2), (T // 2, T))
+        for t0, t1 in halves:
+            apply_gate(last, t0, t1)
+        for t0, t1 in halves:
+            add_and_store(last, t0, t1)

@@ -23,6 +23,8 @@ TILES = N // P
 PAIR = 2
 QUADRANT = 32
 SCALE_ROWS = 4
+EARLY_ROWS = 2
+WARM_UP = 5
 GATE_PAD = 4
 
 
@@ -40,11 +42,11 @@ def tile_mix_sum_and_its_own_gate_kernel(
             engine.memset(plane[:].bitcast(U32), 0)
             return plane
 
-        def load_scales(plane, scales):
+        def load_scales(queue, plane, scales, first_r, end_r):
             rows = scales.bitcast(I32).rearrange("g (q r) c -> r q g c", r=SCALE_ROWS)
-            for r in range(SCALE_ROWS):
+            for r in range(first_r, end_r):
                 dst = plane[r:P:QUADRANT, :].bitcast(I32).rearrange("q (g c) -> q g c", g=PASSES)
-                nc.sync.dma_start(out=dst, in_=rows[r])
+                queue.dma_start(out=dst, in_=rows[r])
 
         def load_bytes(name, src):
             words = sb.tile(list(src.shape), U8, name=name, align_bytes=64)
@@ -62,10 +64,11 @@ def tile_mix_sum_and_its_own_gate_kernel(
         gate = [sb.tile([P, GATE_PAD + T], F32, name="gate%d" % i) for i in range(TILES)]
         gated = [sb.tile([P, T], F32, name="gated%d" % i) for i in range(TILES)]
 
-        xt_plane = new_plane("xt_plane", nc.vector)
+        xt_plane = new_plane("xt_plane", nc.gpsimd)
         xq_plane = new_plane("xq_plane", nc.vector)
         wq_plane = new_plane("wq_plane", nc.gpsimd)
-        wc_plane = new_plane("wc_plane", nc.gpsimd)
+        wc_plane = new_plane("wc_plane", nc.vector)
+        load_scales(nc.gpsimd, wq_plane, wq_scales, 0, EARLY_ROWS)
 
         zero = sb.tile([P, 1], F32, name="zero")
         nc.vector.memset(zero[:], 0.0)
@@ -74,41 +77,36 @@ def tile_mix_sum_and_its_own_gate_kernel(
 
         xt, wa_rows, wq = {}, {}, {}
         xt[0] = load_bytes("xt0", xt_words[0].rearrange("p t j -> p (t j)"))
-        load_scales(xt_plane, xt_scales)
+        load_scales(nc.sync, xt_plane, xt_scales, 0, SCALE_ROWS)
         wa_rows[0] = load_wa(0)
-        load_scales(xq_plane, xq_scales)
+        load_scales(nc.sync, xq_plane, xq_scales, 0, SCALE_ROWS)
         wa_rows[1] = load_wa(1)
-        load_scales(wq_plane, wq_scales)
+        load_scales(nc.sync, wq_plane, wq_scales, EARLY_ROWS, SCALE_ROWS)
         xt[1] = load_bytes("xt1", xt_words[1].rearrange("p t j -> p (t j)"))
         xq = load_bytes("xq", xq_words.rearrange("g p b -> p g b"))
         for h in range(TILES // PAIR):
             cols = wq_words[:, :, h * PAIR * P : (h + 1) * PAIR * P, :]
             wq[h] = load_bytes("wq%d" % h, cols.rearrange("g p n j -> p g (n j)"))
-        load_scales(wc_plane, wc_scales)
+        load_scales(nc.sync, wc_plane, wc_scales, 0, SCALE_ROWS)
         wc = load_bytes("wc", wc_words.rearrange("g p b -> p g b"))
 
-        wa_codes, wa_planes = {}, {}
+        wa_grouped, wa_codes, wa_planes = {}, {}, {}
 
-        def quantise_wa(g):
-            grouped = [
-                sb.tile([P, PAIR * K_PASS], BF16, name="wa_grouped%d_%d" % (g, h), align_bytes=64)
-                for h in range(TILES // PAIR)
-            ]
-            for i in range(TILES):
-                h, u = divmod(i, PAIR)
-                dst = grouped[h][:, u * K_PASS : (u + 1) * K_PASS].rearrange("p (c e j) -> p c j e", e=2, j=PACK)
-                src = wa_rows[g][:, :, i * P : (i + 1) * P].rearrange("p j (c e) -> p c j e", e=2)
-                if u == 0:
-                    nc.vector.tensor_copy(out=dst, in_=src)
-                else:
-                    nc.scalar.copy(out=dst, in_=src)
-            for h in range(TILES // PAIR):
-                codes = sb.tile([P, PAIR * P], U32, name="wa_codes%d_%d" % (g, h), align_bytes=64)
-                plane = sb.tile([P, PAIR * P], U8, name="wa_plane%d_%d" % (g, h), align_bytes=64)
-                nc.vector.quantize_mx(out=codes[:].bitcast(FP8X4), scales=plane[:], in_=grouped[h][:])
-                for u in range(PAIR):
-                    wa_codes[h * PAIR + u, g] = codes[:, u * P : (u + 1) * P]
-                    wa_planes[h * PAIR + u, g] = plane[:, u * P : (u + 1) * P]
+        def group_wa(i, g):
+            grouped = sb.tile([P, K_PASS], BF16, name="wa_grouped%d_%d" % (i, g), align_bytes=64)
+            dst = grouped[:].rearrange("p (c e j) -> p c j e", e=2, j=PACK)
+            src = wa_rows[g][:, :, i * P : (i + 1) * P].rearrange("p j (c e) -> p c j e", e=2)
+            if i % 2 == 0:
+                nc.vector.tensor_copy(out=dst, in_=src)
+            else:
+                nc.scalar.copy(out=dst, in_=src)
+            wa_grouped[i, g] = grouped
+
+        def quantise_wa(i, g):
+            codes = sb.tile([P, P], U32, name="wa_codes%d_%d" % (i, g), align_bytes=64)
+            plane = sb.tile([P, P], U8, name="wa_plane%d_%d" % (i, g), align_bytes=64)
+            nc.vector.quantize_mx(out=codes[:].bitcast(FP8X4), scales=plane[:], in_=wa_grouped[i, g][:])
+            wa_codes[i, g], wa_planes[i, g] = codes, plane
 
         def plane_cols(plane, g, first, width):
             return plane[:, g * T + first : g * T + first + width]
@@ -116,8 +114,8 @@ def tile_mix_sum_and_its_own_gate_kernel(
         def wa_xt(i, g):
             nc.tensor.matmul_mx(
                 out=z[i][:],
-                lhsT=wa_codes[i, g].bitcast(FP8X4),
-                lhsT_scale=wa_planes[i, g],
+                lhsT=wa_codes[i, g][:].bitcast(FP8X4),
+                lhsT_scale=wa_planes[i, g][:],
                 rhs=xt[g][:].bitcast(FP8X4),
                 rhs_scale=plane_cols(xt_plane, g, 0, T),
                 start=(g == 0),
@@ -161,12 +159,28 @@ def tile_mix_sum_and_its_own_gate_kernel(
             )
             nc.sync.dma_start(out=out[i * P : (i + 1) * P, t0:t1], in_=y[:])
 
+        last = TILES - 1
         for g in range(PASSES):
-            quantise_wa(g)
+            group_wa(0, g)
+            for i in range(1, TILES):
+                group_wa(i, g)
+                quantise_wa(i - 1, g)
+            quantise_wa(last, g)
+
+        for w in range(WARM_UP):
+            nc.tensor.matmul_mx(
+                out=s[last][:],
+                lhsT=xt[0][:, : 4 * P].bitcast(FP8X4),
+                lhsT_scale=plane_cols(xt_plane, 0, 0, P),
+                rhs=xt[0][:].bitcast(FP8X4),
+                rhs_scale=plane_cols(xt_plane, 0, 0, T),
+                start=(w == 0),
+                stop=(w == WARM_UP - 1),
+            )
+
+        for g in range(PASSES):
             for i in range(TILES):
                 wa_xt(i, g)
-
-        last = TILES - 1
         for i in range(last):
             wq_xq(i)
         wc_xq(0)

from contextlib import ExitStack

import concourse.mybir as mybir

K, L, T, N = 1024, 1024, 512, 512
FLOPS = 2 * N * T * (K + 2 * L)

F32 = mybir.dt.float32
BF16 = mybir.dt.bfloat16
I32 = mybir.dt.int32
U32 = mybir.dt.uint32
U8 = mybir.dt.uint8
FP8X4 = mybir.dt.float8_e4m3fn_x4
FP4X4 = mybir.dt.float4_e2m1fn_x4
ACT = mybir.ActivationFunctionType
ALU = mybir.AluOpType

P = 128
PACK = 4
K_PASS = P * PACK
PASSES = K // K_PASS
TILES = N // P
PAIR = 2
QUADRANT = 32
SCALE_ROWS = 4
EARLY_ROWS = 2
WARM_UP = 5
GATE_PAD = 4


def tile_mix_sum_and_its_own_gate_kernel(
    tc, xt_words, xt_scales, wa, xq_words, xq_scales, wq_words, wq_scales, wc_words, wc_scales, out
):
    nc = tc.nc
    with ExitStack() as ctx:
        sb = ctx.enter_context(tc.tile_pool(name="sb", bufs=1))
        ps = ctx.enter_context(tc.psum_pool(name="ps", bufs=1))
        ctx.enter_context(tc.manual_schedule())

        def new_plane(name, engine):
            plane = sb.tile([P, PASSES * T], U8, name=name, align_bytes=64)
            engine.memset(plane[:].bitcast(U32), 0)
            return plane

        def load_scales(queue, plane, scales, first_r, end_r):
            rows = scales.bitcast(I32).rearrange("g (q r) c -> r q g c", r=SCALE_ROWS)
            for r in range(first_r, end_r):
                dst = plane[r:P:QUADRANT, :].bitcast(I32).rearrange("q (g c) -> q g c", g=PASSES)
                queue.dma_start(out=dst, in_=rows[r])

        def load_bytes(name, src):
            words = sb.tile(list(src.shape), U8, name=name, align_bytes=64)
            nc.sync.dma_start(out=words[:].bitcast(I32), in_=src.bitcast(I32))
            return words

        def load_wa(g):
            rows = sb.tile([P, PACK, N], F32, name="wa_rows%d" % g)
            src = wa[g * K_PASS : (g + 1) * K_PASS, :].rearrange("(p j) n -> p j n", j=PACK)
            nc.sync.dma_start(out=rows[:], in_=src)
            return rows

        z = [ps.tile([P, T], F32, name="z%d" % i) for i in range(TILES)]
        s = [ps.tile([P, T], F32, name="s%d" % i) for i in range(TILES)]
        gate = [sb.tile([P, GATE_PAD + T], F32, name="gate%d" % i) for i in range(TILES)]
        gated = [sb.tile([P, T], F32, name="gated%d" % i) for i in range(TILES)]

        xt_plane = new_plane("xt_plane", nc.gpsimd)
        xq_plane = new_plane("xq_plane", nc.vector)
        wq_plane = new_plane("wq_plane", nc.gpsimd)
        wc_plane = new_plane("wc_plane", nc.vector)
        load_scales(nc.gpsimd, wq_plane, wq_scales, 0, EARLY_ROWS)

        zero = sb.tile([P, 1], F32, name="zero")
        nc.vector.memset(zero[:], 0.0)
        for i in range(TILES):
            nc.scalar.activation(out=gate[i][:, GATE_PAD - 1 : GATE_PAD], in_=zero[:], func=ACT.Sigmoid)

        xt, wa_rows, wq = {}, {}, {}
        xt[0] = load_bytes("xt0", xt_words[0].rearrange("p t j -> p (t j)"))
        load_scales(nc.sync, xt_plane, xt_scales, 0, SCALE_ROWS)
        wa_rows[0] = load_wa(0)
        load_scales(nc.sync, xq_plane, xq_scales, 0, SCALE_ROWS)
        wa_rows[1] = load_wa(1)
        load_scales(nc.sync, wq_plane, wq_scales, EARLY_ROWS, SCALE_ROWS)
        xt[1] = load_bytes("xt1", xt_words[1].rearrange("p t j -> p (t j)"))
        xq = load_bytes("xq", xq_words.rearrange("g p b -> p g b"))
        for h in range(TILES // PAIR):
            cols = wq_words[:, :, h * PAIR * P : (h + 1) * PAIR * P, :]
            wq[h] = load_bytes("wq%d" % h, cols.rearrange("g p n j -> p g (n j)"))
        load_scales(nc.sync, wc_plane, wc_scales, 0, SCALE_ROWS)
        wc = load_bytes("wc", wc_words.rearrange("g p b -> p g b"))

        wa_grouped, wa_codes, wa_planes = {}, {}, {}

        def group_wa(i, g):
            grouped = sb.tile([P, K_PASS], BF16, name="wa_grouped%d_%d" % (i, g), align_bytes=64)
            dst = grouped[:].rearrange("p (c e j) -> p c j e", e=2, j=PACK)
            src = wa_rows[g][:, :, i * P : (i + 1) * P].rearrange("p j (c e) -> p c j e", e=2)
            if i % 2 == 0:
                nc.vector.tensor_copy(out=dst, in_=src)
            else:
                nc.scalar.copy(out=dst, in_=src)
            wa_grouped[i, g] = grouped

        def quantise_wa(i, g):
            codes = sb.tile([P, P], U32, name="wa_codes%d_%d" % (i, g), align_bytes=64)
            plane = sb.tile([P, P], U8, name="wa_plane%d_%d" % (i, g), align_bytes=64)
            nc.vector.quantize_mx(out=codes[:].bitcast(FP8X4), scales=plane[:], in_=wa_grouped[i, g][:])
            wa_codes[i, g], wa_planes[i, g] = codes, plane

        def plane_cols(plane, g, first, width):
            return plane[:, g * T + first : g * T + first + width]

        def wa_xt(i, g):
            nc.tensor.matmul_mx(
                out=z[i][:],
                lhsT=wa_codes[i, g][:].bitcast(FP8X4),
                lhsT_scale=wa_planes[i, g][:],
                rhs=xt[g][:].bitcast(FP8X4),
                rhs_scale=plane_cols(xt_plane, g, 0, T),
                start=(g == 0),
                stop=False,
            )

        def wq_xq(i):
            h, u = divmod(i, PAIR)
            for g in range(PASSES):
                nc.tensor.matmul_mx(
                    out=z[i][:],
                    lhsT=wq[h][:, g, 4 * u * P : 4 * (u + 1) * P].bitcast(FP8X4),
                    lhsT_scale=plane_cols(wq_plane, g, i * P, P),
                    rhs=xq[:, g, :].bitcast(FP4X4),
                    rhs_scale=plane_cols(xq_plane, g, 0, T),
                    start=False,
                    stop=(g == PASSES - 1),
                )
            nc.scalar.activation(out=gate[i][:, GATE_PAD:], in_=z[i][:], func=ACT.Sigmoid)

        def wc_xq(i):
            for g in range(PASSES):
                nc.tensor.matmul_mx(
                    out=s[i][:],
                    lhsT=wc[:, g, 2 * i * P : 2 * (i + 1) * P].bitcast(FP4X4),
                    lhsT_scale=plane_cols(wc_plane, g, i * P, P),
                    rhs=xq[:, g, :].bitcast(FP4X4),
                    rhs_scale=plane_cols(xq_plane, g, 0, T),
                    start=(g == 0),
                    stop=(g == PASSES - 1),
                )

        def apply_gate(i, t0, t1):
            shifted = gate[i][:, GATE_PAD - 1 + t0 : GATE_PAD - 1 + t1]
            nc.vector.tensor_tensor(out=gated[i][:, t0:t1], in0=z[i][:, t0:t1], in1=shifted, op=ALU.mult)

        def add_and_store(i, t0, t1):
            y = sb.tile([P, t1 - t0], F32, name="y%d_%d" % (i, t0))
            nc.vector.scalar_tensor_tensor(
                out=y[:], in0=s[i][:, t0:t1], scalar=0.5, in1=gated[i][:, t0:t1], op0=ALU.mult, op1=ALU.add
            )
            nc.sync.dma_start(out=out[i * P : (i + 1) * P, t0:t1], in_=y[:])

        last = TILES - 1
        for g in range(PASSES):
            group_wa(0, g)
            for i in range(1, TILES):
                group_wa(i, g)
                quantise_wa(i - 1, g)
            quantise_wa(last, g)

        for w in range(WARM_UP):
            nc.tensor.matmul_mx(
                out=s[last][:],
                lhsT=xt[0][:, : 4 * P].bitcast(FP8X4),
                lhsT_scale=plane_cols(xt_plane, 0, 0, P),
                rhs=xt[0][:].bitcast(FP8X4),
                rhs_scale=plane_cols(xt_plane, 0, 0, T),
                start=(w == 0),
                stop=(w == WARM_UP - 1),
            )

        for g in range(PASSES):
            for i in range(TILES):
                wa_xt(i, g)
        for i in range(last):
            wq_xq(i)
        wc_xq(0)
        wq_xq(last)
        for i in range(1, TILES):
            wc_xq(i)

        apply_gate(0, 0, T)
        for i in range(1, last):
            apply_gate(i, 0, T)
            add_and_store(i - 1, 0, T)
        add_and_store(last - 1, 0, T)
        halves = ((0, T // 2), (T // 2, T))
        for t0, t1 in halves:
            apply_gate(last, t0, t1)
        for t0, t1 in halves:
            add_and_store(last, t0, t1)
